import numpy as np
import ml_dtypes


def mxq(x, axis, fmt="e4m3"):
    dtype, down = {"e4m3": (ml_dtypes.float8_e4m3fn, 7), "e5m2": (ml_dtypes.float8_e5m2, 14)}[fmt]
    v = np.moveaxis(np.asarray(x, np.float32).astype(ml_dtypes.bfloat16).astype(np.float64), axis, -1)
    blocks = v.reshape(v.shape[:-1] + (-1, 32))
    amax = np.abs(blocks).max(-1, keepdims=True)
    byte = np.maximum(np.where(amax > 0, np.frexp(amax)[1] - 1 + 127, 0) - down, 1)
    scale = np.exp2(byte - 127.0)
    codes = (blocks / scale).astype(np.float32).astype(dtype).astype(np.float64)
    return np.moveaxis((codes * scale).reshape(v.shape), -1, axis)


WIDE = False


def mx_kscale(k):
    if not WIDE:
        return np.ones(k)
    levels = np.array([10, -10, 5, -5, 0])
    if k % 512:
        return np.exp2(np.random.permutation(np.resize(levels, k // 32))).repeat(32)
    a = np.empty((k // 512, 16))
    for p in range(k // 512):
        a[p, :8] = np.random.permutation(np.resize(levels, 8))
        for g in range(8):
            far = levels[np.abs(levels - a[p, g]) >= 10]
            a[p, g + 8] = far[np.random.randint(len(far))]
    return np.exp2(a.ravel()).repeat(32)


def f64(x):
    return np.asarray(x).astype(np.float64)


def striped(idx):
    return np.tile(idx.reshape(-1, 16).T, (8, 1)).astype(np.uint16)


def unstriped(offs):
    return offs[:16].T.reshape(-1).astype(np.int64)


def pack_weight(w):
    k, n = w.shape
    w = f64(np.asarray(w, np.float32).astype(ml_dtypes.bfloat16)).reshape(k // 32, 32, n)
    amax = np.abs(w).max(1)
    byte = np.clip(np.where(amax > 0, np.frexp(amax)[1] - 1 + 127 - 7, 1), 1, 254)
    scaled = (w * np.exp2(127.0 - byte)[:, None, :]).reshape(k, n).astype(np.float32)
    words = np.ascontiguousarray(scaled.reshape(k // 512, 128, 4, n).transpose(0, 1, 3, 2)).astype(ml_dtypes.float8_e4m3fn).view(np.uint8)
    return words, np.ascontiguousarray(byte.astype(np.uint8).reshape(k // 512, 16, n))


def unpack_weight(words, scales):
    g, p, n, _ = words.shape
    vals = np.ascontiguousarray(words).view(ml_dtypes.float8_e4m3fn).astype(np.float64) * np.repeat(np.exp2(scales.astype(np.float64) - 127.0), 8, axis=1)[..., None]
    return vals.transpose(0, 1, 3, 2).reshape(g * 512, n)


K, T, E, C, N = 1024, 2048, 4, 128, 256


def by_expert(wq, xq):
    return np.concatenate([wq[e].T @ xq[:, e * C:(e + 1) * C] for e in range(E)], axis=1)


def setup_inputs():
    n = np.random.standard_normal
    s = mx_kscale(K)[:, None]
    packed = [pack_weight(m) for m in n((E, K, N)) / np.sqrt(K) / s[None]]
    return {
        "xT": (n((K, T)) * s).astype(np.float32),
        "w_words": np.stack([m[0] for m in packed]),
        "w_scales": np.stack([m[1] for m in packed]),
        "gate": np.tile(np.random.uniform(0.2, 1.0, E * C), (N, 1)).astype(np.float32),
        "offs": striped(np.random.permutation(T)[:E * C]),
    }


def reference(xT, w_words, w_scales, gate, offs):
    idx = unstriped(offs)
    xq = mxq(f64(xT)[:, idx], 0, "e4m3")
    w = np.stack([unpack_weight(w_words[e], w_scales[e]) for e in range(E)])
    y = by_expert(w, xq)
    out = np.zeros((N, T))
    out[:, idx] = f64(gate) * y
    return out

@@ -1,0 +1,132 @@
+from contextlib import ExitStack
+
+import concourse.mybir as mybir
+
+K, T, E, C, N = 1024, 2048, 4, 128, 256
+FLOPS = 2 * K * N * E * C
+
+F32 = mybir.dt.float32
+BF16 = mybir.dt.bfloat16
+I32 = mybir.dt.int32
+U32 = mybir.dt.uint32
+U16 = mybir.dt.uint16
+U8 = mybir.dt.uint8
+FP8X4 = mybir.dt.float8_e4m3fn_x4
+
+P = 128
+PACK = 4
+PASSES = K // (P * PACK)
+SLOTS = E * C
+HALF = SLOTS // 2
+BLOCKS = N // P
+
+
+def tile_routed_moe_kernel(tc, xT, w_words, w_scales, gate, offs, out):
+    nc = tc.nc
+    with ExitStack() as ctx:
+        keep = ctx.enter_context(tc.tile_pool(name="keep", bufs=1))
+        psum = ctx.enter_context(tc.psum_pool(name="psum", bufs=1))
+
+        offsets = keep.tile([P, SLOTS // 16], U16, name="offsets")
+
+        x_rows = xT.rearrange("(g p t) n -> g p t n", p=P, t=PACK)
+        planes = []
+        for g in range(PASSES):
+            for t in range(PACK):
+                plane = keep.tile([P, T], F32, name="plane%d%d" % (g, t))
+                nc.sync.dma_start(plane[:], x_rows[g, :, t, :])
+                planes.append(plane)
+                if len(planes) == 1:
+                    nc.sync.dma_start(offsets[:], offs)
+
+        w_planes = keep.tile([P, E * PASSES, N], U8, name="w_planes", align_bytes=64)
+        nc.vector.memset(w_planes[:].rearrange("p m n -> p (m n)").bitcast(I32), 0)
+        scale_rows = w_scales.bitcast(I32).rearrange("e a q n -> q (e a) n")
+        for r in range(4):
+            nc.sync.dma_start(w_planes[r:P:32, :, :].bitcast(I32), scale_rows[r:16:4, :, :])
+
+        w_codes = keep.tile([P, E * PASSES, N], I32, name="w_codes", align_bytes=64)
+        code_rows = w_words.rearrange("e a p n r -> e a p (n r)").bitcast(I32).rearrange("e a p n -> p (e a) n")
+        gates = [keep.tile([P, SLOTS], F32, name="gate%d" % b) for b in range(BLOCKS)]
+
+        nc.sync.dma_start(w_codes[:, 0:4, 0:P], code_rows[:, 0:4, 0:P])
+        nc.sync.dma_start(gates[0][:], gate[0:P, :])
+        nc.sync.dma_start(w_codes[:, 4:8, 0:P], code_rows[:, 4:8, 0:P])
+        nc.sync.dma_start(w_codes[:, :, P:N], code_rows[:, :, P:N])
+        nc.sync.dma_start(gates[1][:], gate[P:N, :])
+
+        windows = [keep.tile([P, T], F32, name="window%d" % b) for b in range(BLOCKS)]
+        for b in range(BLOCKS):
+            nc.vector.memset(windows[b][:], 0.0)
+
+        grouped = [keep.tile([P, SLOTS, PACK], BF16, name="grouped%d" % g, align_bytes=64) for g in range(PASSES)]
+        x_codes = [keep.tile([P, SLOTS], U32, name="x_codes%d" % g, align_bytes=64) for g in range(PASSES)]
+        x_planes = [keep.tile([P, SLOTS], U8, name="x_planes%d" % g, align_bytes=64) for g in range(PASSES)]
+
+        raw0 = keep.tile([P, PACK, SLOTS], F32, name="raw0")
+        raw1 = keep.tile([P, 2, SLOTS], F32, name="raw1")
+
+        def gather_plain(g, t, raw):
+            nc.vector.tensor_copy(out=raw[:, t, :], in_=planes[g * PACK + t][:].indirect(offsets[:]))
+
+        def gather(g, t, j0, j1):
+            nc.vector.tensor_copy(
+                out=grouped[g][:, j0:j1, t],
+                in_=planes[g * PACK + t][:].indirect(offsets[:, j0 // 16 : j1 // 16]),
+            )
+
+        def quantise(g, j0, j1):
+            nc.vector.quantize_mx(
+                out=x_codes[g][:, j0:j1].bitcast(FP8X4),
+                scales=x_planes[g][:, j0:j1],
+                in_=grouped[g][:, j0:j1, :].rearrange("p n t -> p (n t)"),
+            )
+
+        for t in range(PACK):
+            gather_plain(0, t, raw0)
+        nc.scalar.copy(out=grouped[0][:], in_=raw0[:].rearrange("p t n -> p n t"))
+        gather_plain(1, 0, raw1)
+        quantise(0, 0, SLOTS)
+        gather_plain(1, 1, raw1)
+        nc.scalar.copy(out=grouped[1][:, :, 0:2], in_=raw1[:].rearrange("p t n -> p n t"))
+        gather(1, 2, 0, SLOTS)
+        for h in range(2):
+            gather(1, PACK - 1, h * HALF, (h + 1) * HALF)
+            quantise(1, h * HALF, (h + 1) * HALF)
+
+        sums = [[psum.tile([P, C], F32, name="sum%d%d" % (b, e)) for e in range(E)] for b in range(BLOCKS)]
+        y = [keep.tile([P, SLOTS], F32, name="y%d" % b) for b in range(BLOCKS)]
+
+        def multiply(b, e, a):
+            m = e * PASSES + a
+            nc.tensor.matmul_mx(
+                out=sums[b][e][:],
+                lhsT=w_codes[:, m, b * P : (b + 1) * P].bitcast(FP8X4),
+                lhsT_scale=w_planes[:, m, b * P : (b + 1) * P],
+                rhs=x_codes[a][:, e * C : (e + 1) * C].bitcast(FP8X4),
+                rhs_scale=x_planes[a][:, e * C : (e + 1) * C],
+                start=(a == 0),
+                stop=(a == PASSES - 1),
+            )
+
+        def scatter(b, j0, j1):
+            nc.vector.tensor_tensor(
+                out=windows[b][:].indirect(offsets[:, j0 // 16 : j1 // 16]),
+                in0=y[b][:, j0:j1],
+                in1=gates[b][:, j0:j1],
+                op=mybir.AluOpType.mult,
+            )
+
+        for b in range(BLOCKS):
+            for h in range(2):
+                experts = (2 * h, 2 * h + 1)
+                for a in range(PASSES):
+                    for e in experts:
+                        multiply(b, e, a)
+                for e in experts:
+                    nc.scalar.copy(out=y[b][:, e * C : (e + 1) * C], in_=sums[b][e][:])
+                if b == 0:
+                    scatter(b, h * HALF, (h + 1) * HALF)
+            if b == 1:
+                scatter(b, 0, SLOTS)
+            nc.sync.dma_start(out[b * P : (b + 1) * P, :], windows[b][:])

@@ -33,7 +33,7 @@ def tile_routed_moe_kernel(tc, xT, w_words, w_scales, gate, offs, out):
         planes = []
         for g in range(PASSES):
             for t in range(PACK):
-                plane = keep.tile([P, T], F32, name="plane%d%d" % (g, t))
+                plane = keep.tile([P, T], F32, name="plane%d%d" % (g, t), align_bytes=256)
                 nc.sync.dma_start(plane[:], x_rows[g, :, t, :])
                 planes.append(plane)
                 if len(planes) == 1:
@@ -55,7 +55,7 @@ def tile_routed_moe_kernel(tc, xT, w_words, w_scales, gate, offs, out):
         nc.sync.dma_start(w_codes[:, :, P:N], code_rows[:, :, P:N])
         nc.sync.dma_start(gates[1][:], gate[P:N, :])
 
-        windows = [keep.tile([P, T], F32, name="window%d" % b) for b in range(BLOCKS)]
+        windows = [keep.tile([P, T], F32, name="window%d" % b, align_bytes=256) for b in range(BLOCKS)]
         for b in range(BLOCKS):
             nc.vector.memset(windows[b][:], 0.0)
 

@@ -30,14 +30,11 @@ def tile_routed_moe_kernel(tc, xT, w_words, w_scales, gate, offs, out):
         offsets = keep.tile([P, SLOTS // 16], U16, name="offsets")
 
         x_rows = xT.rearrange("(g p t) n -> g p t n", p=P, t=PACK)
-        planes = []
-        for g in range(PASSES):
-            for t in range(PACK):
-                plane = keep.tile([P, T], F32, name="plane%d%d" % (g, t), align_bytes=256)
-                nc.sync.dma_start(plane[:], x_rows[g, :, t, :])
-                planes.append(plane)
-                if len(planes) == 1:
-                    nc.sync.dma_start(offsets[:], offs)
+        planes = [keep.tile([P, T], F32, name="plane%d" % i, align_bytes=256) for i in range(PASSES * PACK)]
+        for g, t in [(0, 0), (0, 1), (0, 2), (0, 3), (1, 2), (1, 0), (1, 1), (1, 3)]:
+            nc.sync.dma_start(planes[g * PACK + t][:], x_rows[g, :, t, :])
+            if (g, t) == (0, 0):
+                nc.sync.dma_start(offsets[:], offs)
 
         w_planes = keep.tile([P, E * PASSES, N], U8, name="w_planes", align_bytes=64)
         nc.vector.memset(w_planes[:].rearrange("p m n -> p (m n)").bitcast(I32), 0)
@@ -85,11 +82,13 @@ def tile_routed_moe_kernel(tc, xT, w_words, w_scales, gate, offs, out):
         for t in range(PACK):
             gather_plain(0, t, raw0)
         nc.scalar.copy(out=grouped[0][:], in_=raw0[:].rearrange("p t n -> p n t"))
-        gather_plain(1, 0, raw1)
-        quantise(0, 0, SLOTS)
-        gather_plain(1, 1, raw1)
-        nc.scalar.copy(out=grouped[1][:, :, 0:2], in_=raw1[:].rearrange("p t n -> p n t"))
         gather(1, 2, 0, SLOTS)
+        quantise(0, 0, SLOTS)
+        gather_plain(1, 0, raw1)
+        gather_plain(1, 1, raw1)
+        for h in range(2):
+            half = slice(h * HALF, (h + 1) * HALF)
+            nc.scalar.copy(out=grouped[1][:, half, 0:2], in_=raw1[:, :, half].rearrange("p t n -> p n t"))
         for h in range(2):
             gather(1, PACK - 1, h * HALF, (h + 1) * HALF)
             quantise(1, h * HALF, (h + 1) * HALF)

@@ -31,10 +31,14 @@ def tile_routed_moe_kernel(tc, xT, w_words, w_scales, gate, offs, out):
 
         x_rows = xT.rearrange("(g p t) n -> g p t n", p=P, t=PACK)
         planes = [keep.tile([P, T], F32, name="plane%d" % i, align_bytes=256) for i in range(PASSES * PACK)]
-        for g, t in [(0, 0), (0, 1), (0, 2), (0, 3), (1, 2), (1, 0), (1, 1), (1, 3)]:
+        for g, t in [(0, 0), (0, 1), (0, 2), (0, 3), (1, 0), (1, 1), (1, 2)]:
             nc.sync.dma_start(planes[g * PACK + t][:], x_rows[g, :, t, :])
             if (g, t) == (0, 0):
                 nc.sync.dma_start(offsets[:], offs)
+        last = planes[PASSES * PACK - 1]
+        chunks = [(0, T // 2), (T // 2, T)]
+        for c0, c1 in chunks:
+            nc.sync.dma_start(last[:, c0:c1], x_rows[PASSES - 1, :, PACK - 1, c0:c1])
 
         w_planes = keep.tile([P, E * PASSES, N], U8, name="w_planes", align_bytes=64)
         nc.vector.memset(w_planes[:].rearrange("p m n -> p (m n)").bitcast(I32), 0)
@@ -62,6 +66,8 @@ def tile_routed_moe_kernel(tc, xT, w_words, w_scales, gate, offs, out):
 
         raw0 = keep.tile([P, PACK, SLOTS], F32, name="raw0")
         raw1 = keep.tile([P, 2, SLOTS], F32, name="raw1")
+        raw2 = keep.tile([P, HALF], F32, name="raw2")
+        last16 = keep.tile([P, T], BF16, name="last16", align_bytes=64)
 
         def gather_plain(g, t, raw):
             nc.vector.tensor_copy(out=raw[:, t, :], in_=planes[g * PACK + t][:].indirect(offsets[:]))
@@ -82,15 +88,24 @@ def tile_routed_moe_kernel(tc, xT, w_words, w_scales, gate, offs, out):
         for t in range(PACK):
             gather_plain(0, t, raw0)
         nc.scalar.copy(out=grouped[0][:], in_=raw0[:].rearrange("p t n -> p n t"))
-        gather(1, 2, 0, SLOTS)
-        quantise(0, 0, SLOTS)
         gather_plain(1, 0, raw1)
+        quantise(0, 0, SLOTS)
         gather_plain(1, 1, raw1)
         for h in range(2):
             half = slice(h * HALF, (h + 1) * HALF)
             nc.scalar.copy(out=grouped[1][:, half, 0:2], in_=raw1[:, :, half].rearrange("p t n -> p n t"))
+        nc.vector.tensor_copy(out=raw2[:], in_=planes[PACK + 2][:].indirect(offsets[:, HALF // 16 :]))
+        nc.scalar.copy(out=grouped[1][:, HALF:SLOTS, 2], in_=raw2[:])
+        gather(1, 2, 0, HALF)
+        nc.vector.tensor_copy(out=last16[:, 0 : T // 2], in_=last[:, 0 : T // 2])
+        gather(1, PACK - 1, 0, HALF)
+        nc.scalar.copy(out=last16[:, T // 2 : T], in_=last[:, T // 2 : T])
+        nc.scalar.activation(
+            out=grouped[1][:, HALF:SLOTS, PACK - 1],
+            in_=last16[:].indirect(offsets[:, HALF // 16 :]),
+            func=mybir.ActivationFunctionType.Copy,
+        )
         for h in range(2):
-            gather(1, PACK - 1, h * HALF, (h + 1) * HALF)
             quantise(1, h * HALF, (h + 1) * HALF)
 
         sums = [[psum.tile([P, C], F32, name="sum%d%d" % (b, e)) for e in range(E)] for b in range(BLOCKS)]

@@ -36,7 +36,7 @@ def tile_routed_moe_kernel(tc, xT, w_words, w_scales, gate, offs, out):
             if (g, t) == (0, 0):
                 nc.sync.dma_start(offsets[:], offs)
         last = planes[PASSES * PACK - 1]
-        chunks = [(0, T // 2), (T // 2, T)]
+        chunks = [(0, 1024), (1024, 1536), (1536, T)]
         for c0, c1 in chunks:
             nc.sync.dma_start(last[:, c0:c1], x_rows[PASSES - 1, :, PACK - 1, c0:c1])
 
@@ -50,10 +50,12 @@ def tile_routed_moe_kernel(tc, xT, w_words, w_scales, gate, offs, out):
         code_rows = w_words.rearrange("e a p n r -> e a p (n r)").bitcast(I32).rearrange("e a p n -> p (e a) n")
         gates = [keep.tile([P, SLOTS], F32, name="gate%d" % b) for b in range(BLOCKS)]
 
-        nc.sync.dma_start(w_codes[:, 0:4, 0:P], code_rows[:, 0:4, 0:P])
+        for e in range(2):
+            nc.sync.dma_start(w_codes[:, 2 * e : 2 * e + 2, 0:P], code_rows[:, 2 * e : 2 * e + 2, 0:P])
         nc.sync.dma_start(gates[0][:], gate[0:P, :])
         nc.sync.dma_start(w_codes[:, 4:8, 0:P], code_rows[:, 4:8, 0:P])
-        nc.sync.dma_start(w_codes[:, :, P:N], code_rows[:, :, P:N])
+        for h in range(2):
+            nc.sync.dma_start(w_codes[:, 4 * h : 4 * h + 4, P:N], code_rows[:, 4 * h : 4 * h + 4, P:N])
         nc.sync.dma_start(gates[1][:], gate[P:N, :])
 
         windows = [keep.tile([P, T], F32, name="window%d" % b, align_bytes=256) for b in range(BLOCKS)]
@@ -97,16 +99,17 @@ def tile_routed_moe_kernel(tc, xT, w_words, w_scales, gate, offs, out):
         nc.vector.tensor_copy(out=raw2[:], in_=planes[PACK + 2][:].indirect(offsets[:, HALF // 16 :]))
         nc.scalar.copy(out=grouped[1][:, HALF:SLOTS, 2], in_=raw2[:])
         gather(1, 2, 0, HALF)
-        nc.vector.tensor_copy(out=last16[:, 0 : T // 2], in_=last[:, 0 : T // 2])
+        nc.vector.tensor_copy(out=last16[:, 0:1024], in_=last[:, 0:1024])
+        nc.gpsimd.tensor_copy(out=last16[:, 1024:1536], in_=last[:, 1024:1536])
         gather(1, PACK - 1, 0, HALF)
-        nc.scalar.copy(out=last16[:, T // 2 : T], in_=last[:, T // 2 : T])
+        nc.scalar.copy(out=last16[:, 1536:T], in_=last[:, 1536:T])
         nc.scalar.activation(
             out=grouped[1][:, HALF:SLOTS, PACK - 1],
             in_=last16[:].indirect(offsets[:, HALF // 16 :]),
             func=mybir.ActivationFunctionType.Copy,
         )
-        for h in range(2):
-            quantise(1, h * HALF, (h + 1) * HALF)
+        for j0, j1 in [(0, C), (C, HALF), (HALF, SLOTS)]:
+            quantise(1, j0, j1)
 
         sums = [[psum.tile([P, C], F32, name="sum%d%d" % (b, e)) for e in range(E)] for b in range(BLOCKS)]
         y = [keep.tile([P, SLOTS], F32, name="y%d" % b) for b in range(BLOCKS)]

@@ -31,12 +31,12 @@ def tile_routed_moe_kernel(tc, xT, w_words, w_scales, gate, offs, out):
 
         x_rows = xT.rearrange("(g p t) n -> g p t n", p=P, t=PACK)
         planes = [keep.tile([P, T], F32, name="plane%d" % i, align_bytes=256) for i in range(PASSES * PACK)]
-        for g, t in [(0, 0), (0, 1), (0, 2), (0, 3), (1, 0), (1, 1), (1, 2)]:
+        for g, t in [(0, 0), (0, 1), (0, 2), (0, 3), (1, 2), (1, 0), (1, 1)]:
             nc.sync.dma_start(planes[g * PACK + t][:], x_rows[g, :, t, :])
             if (g, t) == (0, 0):
                 nc.sync.dma_start(offsets[:], offs)
         last = planes[PASSES * PACK - 1]
-        chunks = [(0, 1024), (1024, 1536), (1536, T)]
+        chunks = [(0, 1024), (1024, T)]
         for c0, c1 in chunks:
             nc.sync.dma_start(last[:, c0:c1], x_rows[PASSES - 1, :, PACK - 1, c0:c1])
 
@@ -67,7 +67,6 @@ def tile_routed_moe_kernel(tc, xT, w_words, w_scales, gate, offs, out):
         x_planes = [keep.tile([P, SLOTS], U8, name="x_planes%d" % g, align_bytes=64) for g in range(PASSES)]
 
         raw0 = keep.tile([P, PACK, SLOTS], F32, name="raw0")
-        raw1 = keep.tile([P, 2, SLOTS], F32, name="raw1")
         raw2 = keep.tile([P, HALF], F32, name="raw2")
         last16 = keep.tile([P, T], BF16, name="last16", align_bytes=64)
 
@@ -90,19 +89,16 @@ def tile_routed_moe_kernel(tc, xT, w_words, w_scales, gate, offs, out):
         for t in range(PACK):
             gather_plain(0, t, raw0)
         nc.scalar.copy(out=grouped[0][:], in_=raw0[:].rearrange("p t n -> p n t"))
-        gather_plain(1, 0, raw1)
-        quantise(0, 0, SLOTS)
-        gather_plain(1, 1, raw1)
-        for h in range(2):
-            half = slice(h * HALF, (h + 1) * HALF)
-            nc.scalar.copy(out=grouped[1][:, half, 0:2], in_=raw1[:, :, half].rearrange("p t n -> p n t"))
         nc.vector.tensor_copy(out=raw2[:], in_=planes[PACK + 2][:].indirect(offsets[:, HALF // 16 :]))
         nc.scalar.copy(out=grouped[1][:, HALF:SLOTS, 2], in_=raw2[:])
         gather(1, 2, 0, HALF)
-        nc.vector.tensor_copy(out=last16[:, 0:1024], in_=last[:, 0:1024])
-        nc.gpsimd.tensor_copy(out=last16[:, 1024:1536], in_=last[:, 1024:1536])
+        quantise(0, 0, SLOTS)
+        for t in range(2):
+            nc.vector.tensor_copy(out=grouped[1][:, :, t], in_=planes[PACK + t][:].indirect(offsets[:]))
+        for c in (0, 1024):
+            nc.scalar.copy(out=last16[:, c : c + 512], in_=last[:, c : c + 512])
+            nc.gpsimd.tensor_copy(out=last16[:, c + 512 : c + 1024], in_=last[:, c + 512 : c + 1024])
         gather(1, PACK - 1, 0, HALF)
-        nc.scalar.copy(out=last16[:, 1536:T], in_=last[:, 1536:T])
         nc.scalar.activation(
             out=grouped[1][:, HALF:SLOTS, PACK - 1],
             in_=last16[:].indirect(offsets[:, HALF // 16 :]),

@@ -67,7 +67,7 @@ def tile_routed_moe_kernel(tc, xT, w_words, w_scales, gate, offs, out):
         x_planes = [keep.tile([P, SLOTS], U8, name="x_planes%d" % g, align_bytes=64) for g in range(PASSES)]
 
         raw0 = keep.tile([P, PACK, SLOTS], F32, name="raw0")
-        raw2 = keep.tile([P, HALF], F32, name="raw2")
+        plane16 = keep.tile([P, T], BF16, name="plane16", align_bytes=64)
         last16 = keep.tile([P, T], BF16, name="last16", align_bytes=64)
 
         def gather_plain(g, t, raw):
@@ -86,12 +86,18 @@ def tile_routed_moe_kernel(tc, xT, w_words, w_scales, gate, offs, out):
                 in_=grouped[g][:, j0:j1, :].rearrange("p n t -> p (n t)"),
             )
 
-        for t in range(PACK):
-            gather_plain(0, t, raw0)
-        nc.scalar.copy(out=grouped[0][:], in_=raw0[:].rearrange("p t n -> p n t"))
-        nc.vector.tensor_copy(out=raw2[:], in_=planes[PACK + 2][:].indirect(offsets[:, HALF // 16 :]))
-        nc.scalar.copy(out=grouped[1][:, HALF:SLOTS, 2], in_=raw2[:])
+        for u in (0, 2):
+            for t in (u, u + 1):
+                gather_plain(0, t, raw0)
+            nc.scalar.copy(out=grouped[0][:, :, u : u + 2], in_=raw0[:, u : u + 2, :].rearrange("p t n -> p n t"))
         gather(1, 2, 0, HALF)
+        nc.scalar.copy(out=plane16[:, 0:1024], in_=planes[PACK + 2][:, 0:1024])
+        nc.gpsimd.tensor_copy(out=plane16[:, 1024:T], in_=planes[PACK + 2][:, 1024:T])
+        nc.scalar.activation(
+            out=grouped[1][:, HALF:SLOTS, 2],
+            in_=plane16[:].indirect(offsets[:, HALF // 16 :]),
+            func=mybir.ActivationFunctionType.Copy,
+        )
         quantise(0, 0, SLOTS)
         for t in range(2):
             nc.vector.tensor_copy(out=grouped[1][:, :, t], in_=planes[PACK + t][:].indirect(offsets[:]))

@@ -30,12 +30,14 @@ def tile_routed_moe_kernel(tc, xT, w_words, w_scales, gate, offs, out):
         offsets = keep.tile([P, SLOTS // 16], U16, name="offsets")
 
         x_rows = xT.rearrange("(g p t) n -> g p t n", p=P, t=PACK)
-        planes = [keep.tile([P, T], F32, name="plane%d" % i, align_bytes=256) for i in range(PASSES * PACK)]
-        for g, t in [(0, 0), (0, 1), (0, 2), (0, 3), (1, 2), (1, 0), (1, 1)]:
-            nc.sync.dma_start(planes[g * PACK + t][:], x_rows[g, :, t, :])
-            if (g, t) == (0, 0):
-                nc.sync.dma_start(offsets[:], offs)
-        last = planes[PASSES * PACK - 1]
+        pair = keep.tile([P, 2, T], F32, name="pair", align_bytes=256)
+        nc.sync.dma_start(pair[:], x_rows[0, :, 0:2, :])
+        nc.sync.dma_start(offsets[:], offs)
+        singles = [keep.tile([P, T], F32, name="plane%d" % i, align_bytes=256) for i in range(2, PASSES * PACK)]
+        planes = [pair[:, 0, :], pair[:, 1, :]] + [plane[:] for plane in singles]
+        for g, t in [(0, 2), (0, 3), (1, 2), (1, 0), (1, 1)]:
+            nc.sync.dma_start(planes[g * PACK + t], x_rows[g, :, t, :])
+        last = singles[-1]
         chunks = [(0, 1024), (1024, T)]
         for c0, c1 in chunks:
             nc.sync.dma_start(last[:, c0:c1], x_rows[PASSES - 1, :, PACK - 1, c0:c1])
@@ -54,8 +56,8 @@ def tile_routed_moe_kernel(tc, xT, w_words, w_scales, gate, offs, out):
             nc.sync.dma_start(w_codes[:, 2 * e : 2 * e + 2, 0:P], code_rows[:, 2 * e : 2 * e + 2, 0:P])
         nc.sync.dma_start(gates[0][:], gate[0:P, :])
         nc.sync.dma_start(w_codes[:, 4:8, 0:P], code_rows[:, 4:8, 0:P])
-        for h in range(2):
-            nc.sync.dma_start(w_codes[:, 4 * h : 4 * h + 4, P:N], code_rows[:, 4 * h : 4 * h + 4, P:N])
+        for e in range(E):
+            nc.sync.dma_start(w_codes[:, 2 * e : 2 * e + 2, P:N], code_rows[:, 2 * e : 2 * e + 2, P:N])
         nc.sync.dma_start(gates[1][:], gate[P:N, :])
 
         windows = [keep.tile([P, T], F32, name="window%d" % b, align_bytes=256) for b in range(BLOCKS)]
@@ -71,12 +73,12 @@ def tile_routed_moe_kernel(tc, xT, w_words, w_scales, gate, offs, out):
         last16 = keep.tile([P, T], BF16, name="last16", align_bytes=64)
 
         def gather_plain(g, t, raw):
-            nc.vector.tensor_copy(out=raw[:, t, :], in_=planes[g * PACK + t][:].indirect(offsets[:]))
+            nc.vector.tensor_copy(out=raw[:, t, :], in_=planes[g * PACK + t].indirect(offsets[:]))
 
         def gather(g, t, j0, j1):
             nc.vector.tensor_copy(
                 out=grouped[g][:, j0:j1, t],
-                in_=planes[g * PACK + t][:].indirect(offsets[:, j0 // 16 : j1 // 16]),
+                in_=planes[g * PACK + t].indirect(offsets[:, j0 // 16 : j1 // 16]),
             )
 
         def quantise(g, j0, j1):
@@ -100,7 +102,7 @@ def tile_routed_moe_kernel(tc, xT, w_words, w_scales, gate, offs, out):
         )
         quantise(0, 0, SLOTS)
         for t in range(2):
-            nc.vector.tensor_copy(out=grouped[1][:, :, t], in_=planes[PACK + t][:].indirect(offsets[:]))
+            nc.vector.tensor_copy(out=grouped[1][:, :, t], in_=planes[PACK + t].indirect(offsets[:]))
         for c in (0, 1024):
             nc.scalar.copy(out=last16[:, c : c + 512], in_=last[:, c : c + 512])
             nc.gpsimd.tensor_copy(out=last16[:, c + 512 : c + 1024], in_=last[:, c + 512 : c + 1024])

from contextlib import ExitStack

import concourse.mybir as mybir

K, T, E, C, N = 1024, 2048, 4, 128, 256
FLOPS = 2 * K * N * E * C

F32 = mybir.dt.float32
BF16 = mybir.dt.bfloat16
I32 = mybir.dt.int32
U32 = mybir.dt.uint32
U16 = mybir.dt.uint16
U8 = mybir.dt.uint8
FP8X4 = mybir.dt.float8_e4m3fn_x4

P = 128
PACK = 4
PASSES = K // (P * PACK)
SLOTS = E * C
HALF = SLOTS // 2
BLOCKS = N // P


def tile_routed_moe_kernel(tc, xT, w_words, w_scales, gate, offs, out):
    nc = tc.nc
    with ExitStack() as ctx:
        keep = ctx.enter_context(tc.tile_pool(name="keep", bufs=1))
        psum = ctx.enter_context(tc.psum_pool(name="psum", bufs=1))

        offsets = keep.tile([P, SLOTS // 16], U16, name="offsets")

        x_rows = xT.rearrange("(g p t) n -> g p t n", p=P, t=PACK)
        pair = keep.tile([P, 2, T], F32, name="pair", align_bytes=256)
        nc.sync.dma_start(pair[:], x_rows[0, :, 0:2, :])
        nc.sync.dma_start(offsets[:], offs)
        singles = [keep.tile([P, T], F32, name="plane%d" % i, align_bytes=256) for i in range(2, PASSES * PACK)]
        planes = [pair[:, 0, :], pair[:, 1, :]] + [plane[:] for plane in singles]
        for g, t in [(0, 2), (0, 3), (1, 2), (1, 0), (1, 1)]:
            nc.sync.dma_start(planes[g * PACK + t], x_rows[g, :, t, :])
        last = singles[-1]
        chunks = [(0, 1024), (1024, T)]
        for c0, c1 in chunks:
            nc.sync.dma_start(last[:, c0:c1], x_rows[PASSES - 1, :, PACK - 1, c0:c1])

        w_planes = keep.tile([P, E * PASSES, N], U8, name="w_planes", align_bytes=64)
        nc.vector.memset(w_planes[:].rearrange("p m n -> p (m n)").bitcast(I32), 0)
        scale_rows = w_scales.bitcast(I32).rearrange("e a q n -> q (e a) n")
        for r in range(4):
            nc.sync.dma_start(w_planes[r:P:32, :, :].bitcast(I32), scale_rows[r:16:4, :, :])

        w_codes = keep.tile([P, E * PASSES, N], I32, name="w_codes", align_bytes=64)
        code_rows = w_words.rearrange("e a p n r -> e a p (n r)").bitcast(I32).rearrange("e a p n -> p (e a) n")
        gates = [keep.tile([P, SLOTS], F32, name="gate%d" % b) for b in range(BLOCKS)]

        for e in range(2):
            nc.sync.dma_start(w_codes[:, 2 * e : 2 * e + 2, 0:P], code_rows[:, 2 * e : 2 * e + 2, 0:P])
        nc.sync.dma_start(gates[0][:], gate[0:P, :])
        nc.sync.dma_start(w_codes[:, 4:8, 0:P], code_rows[:, 4:8, 0:P])
        for e in range(E):
            nc.sync.dma_start(w_codes[:, 2 * e : 2 * e + 2, P:N], code_rows[:, 2 * e : 2 * e + 2, P:N])
        nc.sync.dma_start(gates[1][:], gate[P:N, :])

        windows = [keep.tile([P, T], F32, name="window%d" % b, align_bytes=256) for b in range(BLOCKS)]
        for b in range(BLOCKS):
            nc.vector.memset(windows[b][:], 0.0)

        grouped = [keep.tile([P, SLOTS, PACK], BF16, name="grouped%d" % g, align_bytes=64) for g in range(PASSES)]
        x_codes = [keep.tile([P, SLOTS], U32, name="x_codes%d" % g, align_bytes=64) for g in range(PASSES)]
        x_planes = [keep.tile([P, SLOTS], U8, name="x_planes%d" % g, align_bytes=64) for g in range(PASSES)]

        raw0 = keep.tile([P, PACK, SLOTS], F32, name="raw0")
        plane16 = keep.tile([P, T], BF16, name="plane16", align_bytes=64)
        last16 = keep.tile([P, T], BF16, name="last16", align_bytes=64)

        def gather_plain(g, t, raw):
            nc.vector.tensor_copy(out=raw[:, t, :], in_=planes[g * PACK + t].indirect(offsets[:]))

        def gather(g, t, j0, j1):
            nc.vector.tensor_copy(
                out=grouped[g][:, j0:j1, t],
                in_=planes[g * PACK + t].indirect(offsets[:, j0 // 16 : j1 // 16]),
            )

        def quantise(g, j0, j1):
            nc.vector.quantize_mx(
                out=x_codes[g][:, j0:j1].bitcast(FP8X4),
                scales=x_planes[g][:, j0:j1],
                in_=grouped[g][:, j0:j1, :].rearrange("p n t -> p (n t)"),
            )

        for u in (0, 2):
            for t in (u, u + 1):
                gather_plain(0, t, raw0)
            nc.scalar.copy(out=grouped[0][:, :, u : u + 2], in_=raw0[:, u : u + 2, :].rearrange("p t n -> p n t"))
        gather(1, 2, 0, HALF)
        nc.scalar.copy(out=plane16[:, 0:1024], in_=planes[PACK + 2][:, 0:1024])
        nc.gpsimd.tensor_copy(out=plane16[:, 1024:T], in_=planes[PACK + 2][:, 1024:T])
        nc.scalar.activation(
            out=grouped[1][:, HALF:SLOTS, 2],
            in_=plane16[:].indirect(offsets[:, HALF // 16 :]),
            func=mybir.ActivationFunctionType.Copy,
        )
        quantise(0, 0, SLOTS)
        for t in range(2):
            nc.vector.tensor_copy(out=grouped[1][:, :, t], in_=planes[PACK + t].indirect(offsets[:]))
        for c in (0, 1024):
            nc.scalar.copy(out=last16[:, c : c + 512], in_=last[:, c : c + 512])
            nc.gpsimd.tensor_copy(out=last16[:, c + 512 : c + 1024], in_=last[:, c + 512 : c + 1024])
        gather(1, PACK - 1, 0, HALF)
        nc.scalar.activation(
            out=grouped[1][:, HALF:SLOTS, PACK - 1],
            in_=last16[:].indirect(offsets[:, HALF // 16 :]),
            func=mybir.ActivationFunctionType.Copy,
        )
        for j0, j1 in [(0, C), (C, HALF), (HALF, SLOTS)]:
            quantise(1, j0, j1)

        sums = [[psum.tile([P, C], F32, name="sum%d%d" % (b, e)) for e in range(E)] for b in range(BLOCKS)]
        y = [keep.tile([P, SLOTS], F32, name="y%d" % b) for b in range(BLOCKS)]

        def multiply(b, e, a):
            m = e * PASSES + a
            nc.tensor.matmul_mx(
                out=sums[b][e][:],
                lhsT=w_codes[:, m, b * P : (b + 1) * P].bitcast(FP8X4),
                lhsT_scale=w_planes[:, m, b * P : (b + 1) * P],
                rhs=x_codes[a][:, e * C : (e + 1) * C].bitcast(FP8X4),
                rhs_scale=x_planes[a][:, e * C : (e + 1) * C],
                start=(a == 0),
                stop=(a == PASSES - 1),
            )

        def scatter(b, j0, j1):
            nc.vector.tensor_tensor(
                out=windows[b][:].indirect(offsets[:, j0 // 16 : j1 // 16]),
                in0=y[b][:, j0:j1],
                in1=gates[b][:, j0:j1],
                op=mybir.AluOpType.mult,
            )

        for b in range(BLOCKS):
            for h in range(2):
                experts = (2 * h, 2 * h + 1)
                for a in range(PASSES):
                    for e in experts:
                        multiply(b, e, a)
                for e in experts:
                    nc.scalar.copy(out=y[b][:, e * C : (e + 1) * C], in_=sums[b][e][:])
                if b == 0:
                    scatter(b, h * HALF, (h + 1) * HALF)
            if b == 1:
                scatter(b, 0, SLOTS)
            nc.sync.dma_start(out[b * P : (b + 1) * P, :], windows[b][:])
